import numpy as np, ml_dtypes
CORES = [76,84,92,100,108,116,124]
N = 7
import mx_ref
NC, WT = 128, 3
LR = np.float32(2.0 ** -3)
BF = ml_dtypes.bfloat16
def cut(t, i, w=512):
    return t[:, w * i:w * i + w]
def setup_inputs(rng):
    def f(*shape):
        return mx_ref.flush((rng.standard_normal(shape, dtype=np.float32) * np.exp2(rng.integers(-2, 3, shape[:-1] + (1,)))).astype(BF))
    return {"w": f(N, 128, WT * 512), "gr": f(N, 128, WT * 512), "x": f(N, 128, 4 * NC)}
def setup_inputs_blocks(rng):
    d = setup_inputs(rng)
    for k in ("x",): d[k] = mx_ref.spread(d[k], rng, 4)
    for k in ("w", "gr"): d[k] = mx_ref.spread(d[k], rng, 2)
    return d
def setup_inputs_wide(rng):
    d = setup_inputs(rng)
    for k in ("w", "gr", "x"): d[k] = mx_ref.flush((d[k].astype(np.float32) * np.exp2(rng.integers(-4, 5, (N, 1, 1))).astype(np.float32)).astype(BF))
    return d
def setup_inputs_faint(rng):
    d = setup_inputs(rng); d["gr"] = mx_ref.flush((d["gr"].astype(np.float32) * np.float32(2.0 ** -12)).astype(BF))
    return d
def reference(w, gr, x):
    H = [mx_ref.quantize((cut(w[j], i).astype(np.float32) - cut(gr[j], i).astype(np.float32) * LR).astype(BF)) for j in range(N) for i in range(WT)]
    y = np.zeros((N, 128, N * WT * NC), np.float32)
    for r in range(N):
        X = mx_ref.quantize(x[r])
        for b in range(N * WT):
            y[r][:, NC * b:NC * b + NC] = mx_ref.matmul(H[b], X)
    return {"y": y}

@@ -1,0 +1,162 @@
+from concourse.bass import DstId, RemoteDMATransfer
+from concourse.mybir import dt, AluOpType, ActivationFunctionType
+
+N, WT, NC, TW = 7, 3, 128, 512
+CORES = [76, 84, 92, 100, 108, 116, 124]
+ALL = range(128)
+STEP = 2.0 ** -3
+ROADS = [((0, False, 0), (0, True, 0)),
+         (None, (1, True, 1)),
+         ((1, False, 0), (1, True, 0))]
+
+SCRATCH = {
+    "wt": ("sbuf", [128, WT * TW], "bfloat16"),
+    "gt": ("sbuf", [128, WT * TW], "bfloat16"),
+    "st": ("sbuf", [128, WT * TW], "bfloat16"),
+    "vt": ("sbuf", [128, WT * TW], "bfloat16"),
+    "xt": ("sbuf", [128, TW], "bfloat16"),
+    "xq": ("sbuf", [128, NC], "float8_e4m3fn_x4"),
+    "xs": ("sbuf", [128, NC], "uint8"),
+    "codes": ("sbuf", [128, N * WT * NC], "float8_e4m3fn_x4"),
+    "planes": ("sbuf", [128, N * WT * NC], "uint8"),
+    "yt": ("sbuf", [128, N * WT * NC], "float32"),
+    "ps": ("psum", [128, 4096], "float32"),
+}
+SEMAPHORES = (["lw%d" % i for i in range(WT)] + ["lg%d" % i for i in range(WT)] + ["lx", "sc", "vv", "qd", "mm", "ev", "ea", "st", "left"]
+              + ["c%d" % b for b in range(N * WT)] + ["p%d" % b for b in range(N * WT)])
+
+
+def rank_program(g, core, T, topo):
+    rank = T.rank_of(core)
+    left = [0]
+    chips = sorted({topo.chip(c) for c in ALL})
+    on = {ch: [c for c in ALL if topo.chip(c) == ch] for ch in chips}
+    mate = {a: b for a in chips for b in chips if topo.mates(a, b)}
+
+    def role(src, r):
+        if r is None:
+            return src
+        ch = topo.chip(src)
+        return [c for c in on[ch] if c != src and (topo.die(c) != topo.die(src)) == bool(r[0])
+                and topo.may_write(c, on[mate[ch]][0]) == r[1]][r[2]]
+
+    def rot(l, c):
+        return [x for x in l if x > c] + [x for x in l if x < c]
+
+    def hops(j, t):
+        src = CORES[j]
+        peers = rot([c for c in CORES if topo.same_plane(topo.chip(c), topo.chip(src))], src)
+        cross = rot([c for c in CORES if c != src and c not in peers], src)
+        a, b = role(src, ROADS[t][0]), role(src, ROADS[t][1])
+        return [(src, [c for c in (b, a) if c != src]), (b, cross), (a, peers)]
+
+    plans = {(j, t): hops(j, t) for j in range(N) for t in range(WT)}
+
+    def mask_of(s, ds):
+        m = topo.mask(s, ds[0])
+        for d in ds:
+            m &= topo.mask(s, d)
+        if all(topo.chip(d) == topo.chip(s) for d in ds):
+            away = [k for k in ALL if topo.chip(k) != topo.chip(s)]
+            m &= ~topo.mask(s, away[0])
+        return m
+
+    def send(j, t, ds, part):
+        b = WT * j + t
+        ap = T.codes[:, NC * b:NC * b + NC].bitcast(dt.uint8) if part == 0 else T.planes[:, NC * b:NC * b + NC]
+        ids = []
+        for d in ds:
+            q = topo.addr(d)
+            ids.append(DstId(rid=q[0], pnc=q[1]))
+        m = mask_of(core, ds)
+        left[0] += bin(m).count("1")
+        g.remote_dma_fused([RemoteDMATransfer(dst_ids=ids, dma_engine_mask=m, remote_sem=T.sem[("c%d", "p%d")[part] % b],
+                                              srcs=[ap], dsts=[ap for d in ds])], local_sem=T.sem.left)
+
+    got = {}
+    for (j, t), h in plans.items():
+        for s, ds in h:
+            if core in ds:
+                got[j, t] = bin(mask_of(s, ds)).count("1")
+    for t in range(WT):
+        for j in range(N):
+            groups = [ds for s, ds in plans[j, t] if s == core]
+            if not groups:
+                continue
+            if j == rank:
+                g.wait_ge(T.sem.qd, t + 1)
+            for part in (0, 1):
+                if j != rank:
+                    g.wait_ge(T.sem[("c%d", "p%d")[part] % (WT * j + t)], got[j, t])
+                for ds in groups:
+                    send(j, t, ds, part)
+    if left[0]:
+        g.wait_ge(T.sem.left, left[0])
+    if rank is None:
+        return
+
+    for t in range(WT):
+        a, e = TW * t, TW * t + TW
+        g.scalar.dma_start(T.gt[:, a:e], T.gr[:, a:e]).then_inc(T.sem["lg%d" % t], 16)
+        g.sync.dma_start(T.wt[:, a:e], T.w[:, a:e]).then_inc(T.sem["lw%d" % t], 16)
+    g.sync.dma_start(T.xt[:], T.x[:]).then_inc(T.sem.lx, 16)
+
+    half = TW // 2
+    for t in range(WT):
+        a, e = (half if t == 0 else TW * t), TW * t + TW
+        g.scalar.wait_ge(T.sem["lg%d" % t], 16)
+        g.scalar.activation(T.st[:, a:e], T.gt[:, a:e], ActivationFunctionType.Copy, scale=STEP).then_inc(T.sem.sc, 1)
+    nv = 0
+    for t in range(WT):
+        a, e = TW * t, TW * t + TW
+        b = WT * rank + t
+        cuts = [(a, e)]
+        if t == 0:
+            g.vector.wait_ge(T.sem.lg0, 16)
+            g.vector.tensor_scalar(T.st[:, 0:half], T.gt[:, 0:half], STEP, None, AluOpType.mult).then_inc(T.sem.vv, 1)
+            nv += 1
+            g.vector.wait_ge(T.sem.vv, nv)
+            cuts = [(0, half), (half, TW)]
+        g.vector.wait_ge(T.sem["lw%d" % t], 16)
+        for lo, hi in cuts:
+            if (t, lo) != (0, 0):
+                g.vector.wait_ge(T.sem.sc, t + 1)
+            g.vector.tensor_tensor(T.vt[:, lo:hi], T.wt[:, lo:hi], T.st[:, lo:hi], AluOpType.subtract).then_inc(T.sem.vv, 1)
+            nv += 1
+        g.vector.wait_ge(T.sem.vv, nv)
+        g.vector.quantize_mx(T.codes[:, NC * b:NC * b + NC], T.planes[:, NC * b:NC * b + NC], T.vt[:, a:e]).then_inc(T.sem.qd, 1)
+    g.vector.wait_ge(T.sem.lx, 16)
+    g.vector.quantize_mx(T.xq[:], T.xs[:], T.xt[:]).then_inc(T.sem.qd, 1)
+
+    others = [CORES.index(c) for c in rot(CORES, core)][::-1]
+    blocks = [(rank, t) for t in range(WT)] + [(k, t) for t in range(WT) for k in others]
+    g.tensor.wait_ge(T.sem.qd, WT + 1)
+    for n, (j, t) in enumerate(blocks):
+        b = WT * j + t
+        if n >= 8:
+            g.tensor.wait_ge(T.sem[("ev", "ea")[n % 2]], (n - 8) // 2 + 1)
+        if j != rank:
+            g.tensor.wait_ge(T.sem["c%d" % b], got[j, t])
+            g.tensor.wait_ge(T.sem["p%d" % b], got[j, t])
+        k = 512 * (n % 8)
+        g.tensor.matmul_mx(T.ps[:, k:k + NC], T.codes[:, NC * b:NC * b + NC], T.planes[:, NC * b:NC * b + NC],
+                           T.xq[:], T.xs[:], True, True).then_inc(T.sem.mm, 1)
+    stored = 0
+    for n, (j, t) in enumerate(blocks):
+        a, e = NC * (WT * j + t), NC * (WT * j + t) + NC
+        k = 512 * (n % 8)
+        if n % 2 == 0:
+            g.vector.wait_ge(T.sem.mm, n + 1)
+            g.vector.tensor_copy(T.yt[:, a:e], T.ps[:, k:k + NC]).then_inc(T.sem.ev, 1)
+        else:
+            g.scalar.wait_ge(T.sem.mm, n + 1)
+            g.scalar.activation(T.yt[:, a:e], T.ps[:, k:k + NC], ActivationFunctionType.Copy).then_inc(T.sem.ea, 1)
+        if j == rank:
+            if t < WT - 1:
+                continue
+            a = NC * WT * j
+            g.sync.wait_ge(T.sem.ea, 1)
+        g.sync.wait_ge(T.sem[("ev", "ea")[n % 2]], n // 2 + 1)
+        g.sync.dma_start(T.y[:, a:e], T.yt[:, a:e]).then_inc(T.sem.st, 16)
+        stored += 1
+    g.sync.wait_ge(T.sem.st, 16 * stored)

@@ -5,9 +5,10 @@ N, WT, NC, TW = 7, 3, 128, 512
 CORES = [76, 84, 92, 100, 108, 116, 124]
 ALL = range(128)
 STEP = 2.0 ** -3
-ROADS = [((0, False, 0), (0, True, 0)),
-         (None, (1, True, 1)),
-         ((1, False, 0), (1, True, 0))]
+PEER = [[(1, False, 1)], [None], [(1, False, 0), None]]
+CROSS = [[(0, True, 0)], [(0, True, 1)], [(1, True, 0)]]
+FUSED = [False, True, False]
+ORDER = [("p", 1), ("p", 0), ("x", 0), ("p", 2), ("x", 1), ("x", 2)]
 
 SCRATCH = {
     "wt": ("sbuf", [128, WT * TW], "bfloat16"),
@@ -22,7 +23,8 @@ SCRATCH = {
     "yt": ("sbuf", [128, N * WT * NC], "float32"),
     "ps": ("psum", [128, 4096], "float32"),
 }
-SEMAPHORES = (["lw%d" % i for i in range(WT)] + ["lg%d" % i for i in range(WT)] + ["lx", "sc", "vv", "qd", "mm", "ev", "ea", "st", "left"]
+SEMAPHORES = (["lw%d" % i for i in range(WT + 1)] + ["lg%d" % i for i in range(WT + 1)]
+              + ["lx", "sc", "vv", "qd", "mm", "ev", "ea", "sty", "stz", "left"]
               + ["c%d" % b for b in range(N * WT)] + ["p%d" % b for b in range(N * WT)])
 
 
@@ -43,14 +45,22 @@ def rank_program(g, core, T, topo):
     def rot(l, c):
         return [x for x in l if x > c] + [x for x in l if x < c]
 
-    def hops(j, t):
-        src = CORES[j]
-        peers = rot([c for c in CORES if topo.same_plane(topo.chip(c), topo.chip(src))], src)
-        cross = rot([c for c in CORES if c != src and c not in peers], src)
-        a, b = role(src, ROADS[t][0]), role(src, ROADS[t][1])
-        return [(src, [c for c in (b, a) if c != src]), (b, cross), (a, peers)]
+    def peers_of(src):
+        return rot([c for c in CORES if topo.same_plane(topo.chip(c), topo.chip(src))], src)
 
-    plans = {(j, t): hops(j, t) for j in range(N) for t in range(WT)}
+    def cross_of(src):
+        p = peers_of(src)
+        return rot([c for c in CORES if c != src and c not in p], src)
+
+    def roads(j, t):
+        src = CORES[j]
+        out = {}
+        for dests, rs in ((cross_of(src), CROSS[t]), (peers_of(src), PEER[t])):
+            for i, d in enumerate(dests):
+                out.setdefault(role(src, rs[i * len(rs) // len(dests)]), []).append(d)
+        return out
+
+    plans = {(j, t): roads(j, t) for j in range(N) for t in range(WT)}
 
     def mask_of(s, ds):
         m = topo.mask(s, ds[0])
@@ -61,7 +71,7 @@ def rank_program(g, core, T, topo):
             m &= ~topo.mask(s, away[0])
         return m
 
-    def send(j, t, ds, part):
+    def transfer(j, t, ds, part):
         b = WT * j + t
         ap = T.codes[:, NC * b:NC * b + NC].bitcast(dt.uint8) if part == 0 else T.planes[:, NC * b:NC * b + NC]
         ids = []
@@ -70,66 +80,68 @@ def rank_program(g, core, T, topo):
             ids.append(DstId(rid=q[0], pnc=q[1]))
         m = mask_of(core, ds)
         left[0] += bin(m).count("1")
-        g.remote_dma_fused([RemoteDMATransfer(dst_ids=ids, dma_engine_mask=m, remote_sem=T.sem[("c%d", "p%d")[part] % b],
-                                              srcs=[ap], dsts=[ap for d in ds])], local_sem=T.sem.left)
+        return RemoteDMATransfer(dst_ids=ids, dma_engine_mask=m, remote_sem=T.sem[("c%d", "p%d")[part] % b],
+                                 srcs=[ap], dsts=[ap for d in ds])
 
     got = {}
     for (j, t), h in plans.items():
-        for s, ds in h:
+        for s, ds in h.items():
             if core in ds:
                 got[j, t] = bin(mask_of(s, ds)).count("1")
+            if s == core and s != CORES[j]:
+                got[j, t] = bin(mask_of(CORES[j], [s])).count("1")
+
     for t in range(WT):
         for j in range(N):
-            groups = [ds for s, ds in plans[j, t] if s == core]
-            if not groups:
-                continue
+            h = plans[j, t]
             if j == rank:
                 g.wait_ge(T.sem.qd, t + 1)
-            for part in (0, 1):
-                if j != rank:
+                groups = [ds for ds in ([s for s in h if s != core], h.get(core, [])) if ds]
+                calls = [groups] if FUSED[t] else [[ds] for ds in groups]
+                for call in calls:
+                    for part in (1, 0):
+                        g.remote_dma_fused([transfer(j, t, ds, part) for ds in call], local_sem=T.sem.left)
+            elif core in h:
+                for part in (1, 0):
                     g.wait_ge(T.sem[("c%d", "p%d")[part] % (WT * j + t)], got[j, t])
-                for ds in groups:
-                    send(j, t, ds, part)
+                    g.remote_dma_fused([transfer(j, t, h[core], part)], local_sem=T.sem.left)
     if left[0]:
         g.wait_ge(T.sem.left, left[0])
     if rank is None:
         return
 
-    for t in range(WT):
-        a, e = TW * t, TW * t + TW
-        g.scalar.dma_start(T.gt[:, a:e], T.gr[:, a:e]).then_inc(T.sem["lg%d" % t], 16)
-        g.sync.dma_start(T.wt[:, a:e], T.w[:, a:e]).then_inc(T.sem["lw%d" % t], 16)
+    half = TW // 2
+    cuts = [(0, half, 0), (half, TW, WT)] + [(TW * t, TW * t + TW, t) for t in range(1, WT)]
+    for a, e, k in cuts:
+        g.scalar.dma_start(T.gt[:, a:e], T.gr[:, a:e]).then_inc(T.sem["lg%d" % k], 16)
+        g.sync.dma_start(T.wt[:, a:e], T.w[:, a:e]).then_inc(T.sem["lw%d" % k], 16)
     g.sync.dma_start(T.xt[:], T.x[:]).then_inc(T.sem.lx, 16)
 
-    half = TW // 2
-    for t in range(WT):
-        a, e = (half if t == 0 else TW * t), TW * t + TW
-        g.scalar.wait_ge(T.sem["lg%d" % t], 16)
+    for a, e, k in cuts[1:]:
+        g.scalar.wait_ge(T.sem["lg%d" % k], 16)
         g.scalar.activation(T.st[:, a:e], T.gt[:, a:e], ActivationFunctionType.Copy, scale=STEP).then_inc(T.sem.sc, 1)
     nv = 0
-    for t in range(WT):
-        a, e = TW * t, TW * t + TW
-        b = WT * rank + t
-        cuts = [(a, e)]
-        if t == 0:
+    for n, (a, e, k) in enumerate(cuts):
+        if n == 0:
             g.vector.wait_ge(T.sem.lg0, 16)
-            g.vector.tensor_scalar(T.st[:, 0:half], T.gt[:, 0:half], STEP, None, AluOpType.mult).then_inc(T.sem.vv, 1)
+            g.vector.tensor_scalar(T.st[:, a:e], T.gt[:, a:e], STEP, None, AluOpType.mult).then_inc(T.sem.vv, 1)
             nv += 1
             g.vector.wait_ge(T.sem.vv, nv)
-            cuts = [(0, half), (half, TW)]
-        g.vector.wait_ge(T.sem["lw%d" % t], 16)
-        for lo, hi in cuts:
-            if (t, lo) != (0, 0):
-                g.vector.wait_ge(T.sem.sc, t + 1)
-            g.vector.tensor_tensor(T.vt[:, lo:hi], T.wt[:, lo:hi], T.st[:, lo:hi], AluOpType.subtract).then_inc(T.sem.vv, 1)
-            nv += 1
-        g.vector.wait_ge(T.sem.vv, nv)
-        g.vector.quantize_mx(T.codes[:, NC * b:NC * b + NC], T.planes[:, NC * b:NC * b + NC], T.vt[:, a:e]).then_inc(T.sem.qd, 1)
+        else:
+            g.vector.wait_ge(T.sem.sc, n)
+        g.vector.wait_ge(T.sem["lw%d" % k], 16)
+        g.vector.tensor_tensor(T.vt[:, a:e], T.wt[:, a:e], T.st[:, a:e], AluOpType.subtract).then_inc(T.sem.vv, 1)
+        nv += 1
+        if e % TW == 0:
+            b = WT * rank + e // TW - 1
+            g.vector.wait_ge(T.sem.vv, nv)
+            g.vector.quantize_mx(T.codes[:, NC * b:NC * b + NC], T.planes[:, NC * b:NC * b + NC],
+                                 T.vt[:, e - TW:e]).then_inc(T.sem.qd, 1)
     g.vector.wait_ge(T.sem.lx, 16)
     g.vector.quantize_mx(T.xq[:], T.xs[:], T.xt[:]).then_inc(T.sem.qd, 1)
 
-    others = [CORES.index(c) for c in rot(CORES, core)][::-1]
-    blocks = [(rank, t) for t in range(WT)] + [(k, t) for t in range(WT) for k in others]
+    froms = {"p": [CORES.index(c) for c in peers_of(core)][::-1], "x": [CORES.index(c) for c in cross_of(core)][::-1]}
+    blocks = [(rank, t) for t in range(WT)] + [(k, t) for f, t in ORDER for k in froms[f]]
     g.tensor.wait_ge(T.sem.qd, WT + 1)
     for n, (j, t) in enumerate(blocks):
         b = WT * j + t
@@ -141,7 +153,8 @@ def rank_program(g, core, T, topo):
         k = 512 * (n % 8)
         g.tensor.matmul_mx(T.ps[:, k:k + NC], T.codes[:, NC * b:NC * b + NC], T.planes[:, NC * b:NC * b + NC],
                            T.xq[:], T.xs[:], True, True).then_inc(T.sem.mm, 1)
-    stored = 0
+
+    stored = [0, 0]
     for n, (j, t) in enumerate(blocks):
         a, e = NC * (WT * j + t), NC * (WT * j + t) + NC
         k = 512 * (n % 8)
@@ -151,12 +164,14 @@ def rank_program(g, core, T, topo):
         else:
             g.scalar.wait_ge(T.sem.mm, n + 1)
             g.scalar.activation(T.yt[:, a:e], T.ps[:, k:k + NC], ActivationFunctionType.Copy).then_inc(T.sem.ea, 1)
+        q = (g.sync, g.scalar)[n % 2]
         if j == rank:
             if t < WT - 1:
                 continue
             a = NC * WT * j
-            g.sync.wait_ge(T.sem.ea, 1)
-        g.sync.wait_ge(T.sem[("ev", "ea")[n % 2]], n // 2 + 1)
-        g.sync.dma_start(T.y[:, a:e], T.yt[:, a:e]).then_inc(T.sem.st, 16)
-        stored += 1
-    g.sync.wait_ge(T.sem.st, 16 * stored)
+            q.wait_ge(T.sem.ea, 1)
+        q.wait_ge(T.sem[("ev", "ea")[n % 2]], n // 2 + 1)
+        q.dma_start(T.y[:, a:e], T.yt[:, a:e]).then_inc(T.sem[("sty", "stz")[n % 2]], 16)
+        stored[n % 2] += 1
+    g.sync.wait_ge(T.sem.sty, 16 * stored[0])
+    g.scalar.wait_ge(T.sem.stz, 16 * stored[1])

from concourse.bass import DstId, RemoteDMATransfer
from concourse.mybir import dt, AluOpType, ActivationFunctionType

N, WT, NC, TW = 7, 3, 128, 512
CORES = [76, 84, 92, 100, 108, 116, 124]
ALL = range(128)
STEP = 2.0 ** -3
PEER = [[(1, False, 1)], [None], [(1, False, 0), None]]
CROSS = [[(0, True, 0)], [(0, True, 1)], [(1, True, 0)]]
FUSED = [False, True, False]
ORDER = [("p", 1), ("p", 0), ("x", 0), ("p", 2), ("x", 1), ("x", 2)]

SCRATCH = {
    "wt": ("sbuf", [128, WT * TW], "bfloat16"),
    "gt": ("sbuf", [128, WT * TW], "bfloat16"),
    "st": ("sbuf", [128, WT * TW], "bfloat16"),
    "vt": ("sbuf", [128, WT * TW], "bfloat16"),
    "xt": ("sbuf", [128, TW], "bfloat16"),
    "xq": ("sbuf", [128, NC], "float8_e4m3fn_x4"),
    "xs": ("sbuf", [128, NC], "uint8"),
    "codes": ("sbuf", [128, N * WT * NC], "float8_e4m3fn_x4"),
    "planes": ("sbuf", [128, N * WT * NC], "uint8"),
    "yt": ("sbuf", [128, N * WT * NC], "float32"),
    "ps": ("psum", [128, 4096], "float32"),
}
SEMAPHORES = (["lw%d" % i for i in range(WT + 1)] + ["lg%d" % i for i in range(WT + 1)]
              + ["lx", "sc", "vv", "qd", "mm", "ev", "ea", "sty", "stz", "left"]
              + ["c%d" % b for b in range(N * WT)] + ["p%d" % b for b in range(N * WT)])


def rank_program(g, core, T, topo):
    rank = T.rank_of(core)
    left = [0]
    chips = sorted({topo.chip(c) for c in ALL})
    on = {ch: [c for c in ALL if topo.chip(c) == ch] for ch in chips}
    mate = {a: b for a in chips for b in chips if topo.mates(a, b)}

    def role(src, r):
        if r is None:
            return src
        ch = topo.chip(src)
        return [c for c in on[ch] if c != src and (topo.die(c) != topo.die(src)) == bool(r[0])
                and topo.may_write(c, on[mate[ch]][0]) == r[1]][r[2]]

    def rot(l, c):
        return [x for x in l if x > c] + [x for x in l if x < c]

    def peers_of(src):
        return rot([c for c in CORES if topo.same_plane(topo.chip(c), topo.chip(src))], src)

    def cross_of(src):
        p = peers_of(src)
        return rot([c for c in CORES if c != src and c not in p], src)

    def roads(j, t):
        src = CORES[j]
        out = {}
        for dests, rs in ((cross_of(src), CROSS[t]), (peers_of(src), PEER[t])):
            for i, d in enumerate(dests):
                out.setdefault(role(src, rs[i * len(rs) // len(dests)]), []).append(d)
        return out

    plans = {(j, t): roads(j, t) for j in range(N) for t in range(WT)}

    def mask_of(s, ds):
        m = topo.mask(s, ds[0])
        for d in ds:
            m &= topo.mask(s, d)
        if all(topo.chip(d) == topo.chip(s) for d in ds):
            away = [k for k in ALL if topo.chip(k) != topo.chip(s)]
            m &= ~topo.mask(s, away[0])
        return m

    def transfer(j, t, ds, part):
        b = WT * j + t
        ap = T.codes[:, NC * b:NC * b + NC].bitcast(dt.uint8) if part == 0 else T.planes[:, NC * b:NC * b + NC]
        ids = []
        for d in ds:
            q = topo.addr(d)
            ids.append(DstId(rid=q[0], pnc=q[1]))
        m = mask_of(core, ds)
        left[0] += bin(m).count("1")
        return RemoteDMATransfer(dst_ids=ids, dma_engine_mask=m, remote_sem=T.sem[("c%d", "p%d")[part] % b],
                                 srcs=[ap], dsts=[ap for d in ds])

    got = {}
    for (j, t), h in plans.items():
        for s, ds in h.items():
            if core in ds:
                got[j, t] = bin(mask_of(s, ds)).count("1")
            if s == core and s != CORES[j]:
                got[j, t] = bin(mask_of(CORES[j], [s])).count("1")

    for t in range(WT):
        for j in range(N):
            h = plans[j, t]
            if j == rank:
                g.wait_ge(T.sem.qd, t + 1)
                groups = [ds for ds in ([s for s in h if s != core], h.get(core, [])) if ds]
                calls = [groups] if FUSED[t] else [[ds] for ds in groups]
                for call in calls:
                    for part in (1, 0):
                        g.remote_dma_fused([transfer(j, t, ds, part) for ds in call], local_sem=T.sem.left)
            elif core in h:
                for part in (1, 0):
                    g.wait_ge(T.sem[("c%d", "p%d")[part] % (WT * j + t)], got[j, t])
                    g.remote_dma_fused([transfer(j, t, h[core], part)], local_sem=T.sem.left)
    if left[0]:
        g.wait_ge(T.sem.left, left[0])
    if rank is None:
        return

    half = TW // 2
    cuts = [(0, half, 0), (half, TW, WT)] + [(TW * t, TW * t + TW, t) for t in range(1, WT)]
    for a, e, k in cuts:
        g.scalar.dma_start(T.gt[:, a:e], T.gr[:, a:e]).then_inc(T.sem["lg%d" % k], 16)
        g.sync.dma_start(T.wt[:, a:e], T.w[:, a:e]).then_inc(T.sem["lw%d" % k], 16)
    g.sync.dma_start(T.xt[:], T.x[:]).then_inc(T.sem.lx, 16)

    for a, e, k in cuts[1:]:
        g.scalar.wait_ge(T.sem["lg%d" % k], 16)
        g.scalar.activation(T.st[:, a:e], T.gt[:, a:e], ActivationFunctionType.Copy, scale=STEP).then_inc(T.sem.sc, 1)
    nv = 0
    for n, (a, e, k) in enumerate(cuts):
        if n == 0:
            g.vector.wait_ge(T.sem.lg0, 16)
            g.vector.tensor_scalar(T.st[:, a:e], T.gt[:, a:e], STEP, None, AluOpType.mult).then_inc(T.sem.vv, 1)
            nv += 1
            g.vector.wait_ge(T.sem.vv, nv)
        else:
            g.vector.wait_ge(T.sem.sc, n)
        g.vector.wait_ge(T.sem["lw%d" % k], 16)
        g.vector.tensor_tensor(T.vt[:, a:e], T.wt[:, a:e], T.st[:, a:e], AluOpType.subtract).then_inc(T.sem.vv, 1)
        nv += 1
        if e % TW == 0:
            b = WT * rank + e // TW - 1
            g.vector.wait_ge(T.sem.vv, nv)
            g.vector.quantize_mx(T.codes[:, NC * b:NC * b + NC], T.planes[:, NC * b:NC * b + NC],
                                 T.vt[:, e - TW:e]).then_inc(T.sem.qd, 1)
    g.vector.wait_ge(T.sem.lx, 16)
    g.vector.quantize_mx(T.xq[:], T.xs[:], T.xt[:]).then_inc(T.sem.qd, 1)

    froms = {"p": [CORES.index(c) for c in peers_of(core)][::-1], "x": [CORES.index(c) for c in cross_of(core)][::-1]}
    blocks = [(rank, t) for t in range(WT)] + [(k, t) for f, t in ORDER for k in froms[f]]
    g.tensor.wait_ge(T.sem.qd, WT + 1)
    for n, (j, t) in enumerate(blocks):
        b = WT * j + t
        if n >= 8:
            g.tensor.wait_ge(T.sem[("ev", "ea")[n % 2]], (n - 8) // 2 + 1)
        if j != rank:
            g.tensor.wait_ge(T.sem["c%d" % b], got[j, t])
            g.tensor.wait_ge(T.sem["p%d" % b], got[j, t])
        k = 512 * (n % 8)
        g.tensor.matmul_mx(T.ps[:, k:k + NC], T.codes[:, NC * b:NC * b + NC], T.planes[:, NC * b:NC * b + NC],
                           T.xq[:], T.xs[:], True, True).then_inc(T.sem.mm, 1)

    stored = [0, 0]
    for n, (j, t) in enumerate(blocks):
        a, e = NC * (WT * j + t), NC * (WT * j + t) + NC
        k = 512 * (n % 8)
        if n % 2 == 0:
            g.vector.wait_ge(T.sem.mm, n + 1)
            g.vector.tensor_copy(T.yt[:, a:e], T.ps[:, k:k + NC]).then_inc(T.sem.ev, 1)
        else:
            g.scalar.wait_ge(T.sem.mm, n + 1)
            g.scalar.activation(T.yt[:, a:e], T.ps[:, k:k + NC], ActivationFunctionType.Copy).then_inc(T.sem.ea, 1)
        q = (g.sync, g.scalar)[n % 2]
        if j == rank:
            if t < WT - 1:
                continue
            a = NC * WT * j
            q.wait_ge(T.sem.ea, 1)
        q.wait_ge(T.sem[("ev", "ea")[n % 2]], n // 2 + 1)
        q.dma_start(T.y[:, a:e], T.yt[:, a:e]).then_inc(T.sem[("sty", "stz")[n % 2]], 16)
        stored[n % 2] += 1
    g.sync.wait_ge(T.sem.sty, 16 * stored[0])
    g.scalar.wait_ge(T.sem.stz, 16 * stored[1])
